import numpy as np
import ml_dtypes


def mxq(x, axis, fmt="e4m3"):
    dtype, down = {"e4m3": (ml_dtypes.float8_e4m3fn, 7), "e5m2": (ml_dtypes.float8_e5m2, 14)}[fmt]
    v = np.moveaxis(np.asarray(x, np.float32).astype(ml_dtypes.bfloat16).astype(np.float64), axis, -1)
    blocks = v.reshape(v.shape[:-1] + (-1, 32))
    amax = np.abs(blocks).max(-1, keepdims=True)
    byte = np.maximum(np.where(amax > 0, np.frexp(amax)[1] - 1 + 127, 0) - down, 1)
    scale = np.exp2(byte - 127.0)
    codes = (blocks / scale).astype(np.float32).astype(dtype).astype(np.float64)
    return np.moveaxis((codes * scale).reshape(v.shape), -1, axis)


WIDE = False


def mx_kscale(k):
    if not WIDE:
        return np.ones(k)
    levels = np.array([10, -10, 5, -5, 0])
    if k % 512:
        return np.exp2(np.random.permutation(np.resize(levels, k // 32))).repeat(32)
    a = np.empty((k // 512, 16))
    for p in range(k // 512):
        a[p, :8] = np.random.permutation(np.resize(levels, 8))
        for g in range(8):
            far = levels[np.abs(levels - a[p, g]) >= 10]
            a[p, g + 8] = far[np.random.randint(len(far))]
    return np.exp2(a.ravel()).repeat(32)


def f64(x):
    return np.asarray(x).astype(np.float64)


def striped(idx):
    return np.tile(idx.reshape(-1, 16).T, (8, 1)).astype(np.uint16)


def unstriped(offs):
    return offs[:16].T.reshape(-1).astype(np.int64)


def striped8(idx):
    return np.concatenate([x.reshape(-1, 16).T for x in idx]).astype(np.uint16)


def runs(offs, k):
    lists = np.stack([offs[16 * r : 16 * r + 16].T.reshape(-1) for r in range(8)]).astype(np.int64)
    return lists[np.arange(k) % 512 // 64]


def pack_weight(w):
    k, n = w.shape
    w = f64(np.asarray(w, np.float32).astype(ml_dtypes.bfloat16)).reshape(k // 32, 32, n)
    amax = np.abs(w).max(1)
    byte = np.clip(np.where(amax > 0, np.frexp(amax)[1] - 1 + 127 - 7, 1), 1, 254)
    scaled = (w * np.exp2(127.0 - byte)[:, None, :]).reshape(k, n).astype(np.float32)
    words = np.ascontiguousarray(scaled.reshape(k // 512, 128, 4, n).transpose(0, 1, 3, 2)).astype(ml_dtypes.float8_e4m3fn).view(np.uint8)
    return words, np.ascontiguousarray(byte.astype(np.uint8).reshape(k // 512, 16, n))


def unpack_weight(words, scales):
    g, p, n, _ = words.shape
    vals = np.ascontiguousarray(words).view(ml_dtypes.float8_e4m3fn).astype(np.float64) * np.repeat(np.exp2(scales.astype(np.float64) - 127.0), 8, axis=1)[..., None]
    return vals.transpose(0, 1, 3, 2).reshape(g * 512, n)


E2M1 = np.array([0.0, 0.5, 1.0, 1.5, 2.0, 3.0, 4.0, 6.0, -0.0, -0.5, -1.0, -1.5, -2.0, -3.0, -4.0, -6.0])


def pack_fp4(w):
    k, n = w.shape
    w = f64(np.asarray(w, np.float32).astype(ml_dtypes.bfloat16)).reshape(k // 32, 32, n)
    amax = np.abs(w).max(1)
    mant, ex = np.frexp(amax / 6.0)
    byte = np.clip(np.where(amax > 0, np.where(mant > 0.5, ex, ex - 1) + 127, 1), 1, 254)
    scaled = (w * np.exp2(127.0 - byte)[:, None, :]).reshape(k, n).astype(np.float32)
    c = np.ascontiguousarray(scaled.reshape(k // 512, 128, 4, n).transpose(0, 1, 3, 2)).astype(ml_dtypes.float4_e2m1fn).view(np.uint8) & 0xF
    words = (c[..., 0::2] | (c[..., 1::2] << 4)).reshape(k // 512, 128, 2 * n)
    return np.ascontiguousarray(words), np.ascontiguousarray(byte.astype(np.uint8).reshape(k // 512, 16, n))


def unpack_fp4(words, scales):
    g, _, n = scales.shape
    words = np.ascontiguousarray(words).reshape(g, 128, n, 2)
    nib = np.empty((g, 128, n, 4), np.uint8)
    nib[..., 0::2] = words & 0xF
    nib[..., 1::2] = words >> 4
    vals = E2M1[nib] * np.repeat(np.exp2(scales.astype(np.float64) - 127.0), 8, axis=1)[..., None]
    return vals.transpose(0, 1, 3, 2).reshape(g * 512, n)


def planes(y):
    n, m = y.shape
    v = y.astype(np.float32).astype(ml_dtypes.bfloat16).astype(np.float64).reshape(n // 32, 32, m)
    top = np.abs(v).max(1)
    byte = np.clip(np.where(top > 0, np.frexp(top)[1] - 1 + 127 - 7, 1), 1, 254)
    codes = (v * np.exp2(127.0 - byte)[:, None, :]).reshape(n, m).astype(np.float32).astype(ml_dtypes.float8_e4m3fn).view(np.uint8)
    words = codes.reshape(n // 512, 128, 4, m).transpose(0, 1, 3, 2)
    return np.ascontiguousarray(words), np.ascontiguousarray(byte.astype(np.uint8).reshape(n // 512, 16, m))


K, T, S, H, C = 512, 2048, 512, 512, 512


def setup_inputs():
    n = np.random.standard_normal
    s = mx_kscale(K)[:, None]
    packed_xT = pack_weight(n((K, T)) * s)
    packed_w1 = pack_fp4(n((K, H)) / np.sqrt(K) / s)
    return {
        "x_words": packed_xT[0],
        "x_scales": packed_xT[1],
        "w1_words": packed_w1[0],
        "w1_scales": packed_w1[1],
        "gs": (np.random.uniform(0.5, 1.5, (K, 1)) / s).astype(np.float32),
        "offs": striped(np.random.permutation(T)[:S]),
        "n1": striped8(np.stack([np.random.permutation(S) for _ in range(8)])),
        "n2": striped8(np.stack([np.random.permutation(S) for _ in range(8)])),
        "ca": striped(np.random.permutation(T)[:C]),
        "cb": striped(np.random.permutation(T)[:C]),
        "n3": striped8(np.stack([np.random.permutation(S) for _ in range(8)])),
        "n4": striped8(np.stack([np.random.permutation(S) for _ in range(8)])),
    }


def reference(x_words, x_scales, w1_words, w1_scales, gs, offs, n1, n2, ca, cb, n3, n4):
    x_ca = unpack_weight(x_words, x_scales)[:, unstriped(ca)]
    xq = unpack_weight(x_words, x_scales)[:, unstriped(offs)]
    y = unpack_fp4(w1_words, w1_scales).T @ xq
    z = f64(gs) * ((y - (y[np.arange(H)[:, None], runs(n1, H)])) / (np.abs(y[np.arange(H)[:, None], runs(n2, H)] - y) + 0.5))
    zq = mxq(z, 0, "e4m3")
    a = 0.0625 * (x_ca.T @ zq)
    x_cb = unpack_weight(x_words, x_scales)[:, unstriped(cb)]
    b = 0.0625 * (x_cb.T @ zq)
    out_0 = a[np.arange(C)[:, None], runs(n3, C)] - (np.tanh(b) * (b[np.arange(C)[:, None], runs(n4, C)]))
    return (out_0,) + planes(out_0)

@@ -1,0 +1,210 @@
+from contextlib import ExitStack
+
+import concourse.mybir as mybir
+
+K, T, S, H, C = 512, 2048, 512, 512, 512
+FLOPS = 2 * K * H * S + 2 * 2 * K * C * S
+
+F32 = mybir.dt.float32
+BF16 = mybir.dt.bfloat16
+I32 = mybir.dt.int32
+U32 = mybir.dt.uint32
+U16 = mybir.dt.uint16
+U8 = mybir.dt.uint8
+FP8X4 = mybir.dt.float8_e4m3fn_x4
+FP4X4 = mybir.dt.float4_e2m1fn_x4
+ALU = mybir.AluOpType
+ACT = mybir.ActivationFunctionType
+
+P = 128
+PACK = 4
+QUADS = 4
+HALF = S // 2
+RUN = 4
+TINY = 1e-37
+
+
+def load_scale_rows(queue, plane, rows):
+    for q in range(QUADS):
+        queue.dma_start(out=plane[32 * q : 32 * q + 4, :].bitcast(I32), in_=rows[4 * q : 4 * q + 4, :].bitcast(I32))
+
+
+def deal(nc, dealt, plain):
+    nc.vector.tensor_copy(
+        out=dealt.rearrange("p (t m) -> p t m", t=PACK),
+        in_=plain.rearrange("p (m t) -> p t m", t=PACK),
+    )
+
+
+def woven(ap):
+    return ap.rearrange("p (c i t) -> p c t i", i=RUN, t=PACK)
+
+
+def planes_walk(ap):
+    return ap.rearrange("p t (c i) -> p c t i", i=RUN)
+
+
+def tile_picked_ccmpsoftbfrac_none_po_kernel(
+    tc, x_words, x_scales, w1_words, w1_scales, gs, offs, n1, n2, ca, cb, n3, n4, out_0, out_1, out_2
+):
+    nc = tc.nc
+    with ExitStack() as ctx:
+        keep = ctx.enter_context(tc.tile_pool(name="keep", bufs=1))
+        ring = ctx.enter_context(tc.tile_pool(name="ring", bufs=2))
+        psum = ctx.enter_context(tc.psum_pool(name="psum", bufs=1))
+
+        def list_tile(name, src):
+            t = keep.tile([P, S // 16], U16, name=name)
+            nc.sync.dma_start(t[:], src)
+            return t
+
+        xs = keep.tile([P, T], U8, align_bytes=64)
+        w1s = keep.tile([P, H], U8, align_bytes=64, tag="w1s")
+        nc.vector.memset(xs[:].bitcast(I32), 0)
+        nc.vector.memset(w1s[:].bitcast(I32), 0)
+        load_scale_rows(nc.scalar, xs, x_scales[0])
+        l_offs = list_tile("l_offs", offs)
+        w1w = keep.tile([P, 2 * H], U8, align_bytes=64, tag="w1w")
+        nc.sync.dma_start(out=w1w[:].bitcast(I32), in_=w1_words[0].bitcast(I32))
+        xw = keep.tile([P, T], U32, align_bytes=64)
+        nc.sync.dma_start(out=xw[:].bitcast(I32), in_=x_words[0].rearrange("p n t -> p (n t)").bitcast(I32))
+        l_ca = list_tile("l_ca", ca)
+        load_scale_rows(nc.scalar, w1s, w1_scales[0])
+        gain = keep.tile([P, PACK], F32)
+        nc.sync.dma_start(out=gain[:], in_=gs.rearrange("(p t) o -> p (t o)", t=PACK))
+        l_cb = list_tile("l_cb", cb)
+        l_n2 = list_tile("l_n2", n2)
+        l_n1 = list_tile("l_n1", n1)
+        l_n4 = list_tile("l_n4", n4)
+        l_n3 = list_tile("l_n3", n3)
+
+        half_c = keep.tile([P, 1], F32)
+        nc.vector.memset(half_c[:], 0.5)
+        win = [keep.tile([P, 2 * S], F32, name=f"win{t}") for t in range(PACK)]
+        for t in range(PACK):
+            nc.vector.memset(win[t][:, S:], 0.0)
+
+        def gather(name, dtype, table, lst, tag=""):
+            g = keep.tile([P, S], dtype, name=name, align_bytes=64, tag=tag or name)
+            nc.vector.tensor_copy(out=g[:], in_=table[:].indirect(lst[:]))
+            return g
+
+        def dealt(name, dtype, plain):
+            d = keep.tile([P, S], dtype, name=name, align_bytes=64)
+            deal(nc, d[:], plain[:])
+            return d
+
+        qs = gather("qs", U8, xs, l_offs)
+        w1d = keep.tile([P, 2 * H], U8, align_bytes=64)
+        nc.vector.tensor_copy(
+            out=w1d[:].rearrange("p (t m b) -> p t m b", t=PACK, b=2),
+            in_=w1w[:].rearrange("p (m t b) -> p t m b", t=PACK, b=2),
+        )
+        w1sd = dealt("w1sd", U8, w1s)
+        qw = gather("qw", U32, xw, l_offs)
+
+        neg_gain = keep.tile([P, PACK], F32)
+        nc.vector.tensor_scalar(neg_gain[:], gain[:], -1.0, None, ALU.mult)
+        abs_gain = keep.tile([P, PACK], F32)
+        nc.vector.scalar_tensor_tensor(abs_gain[:], gain[:], TINY, neg_gain[:], ALU.max, ALU.max)
+        root_gain = keep.tile([P, PACK], F32)
+        nc.scalar.activation(root_gain[:], abs_gain[:], ACT.Abs_reciprocal_sqrt)
+        inv_gain = keep.tile([P, PACK], F32)
+        nc.scalar.activation(inv_gain[:], root_gain[:], ACT.Square)
+
+        banks = [psum.tile([P, S], F32, name=f"y{t}", tag=f"ya{t}") for t in range(PACK)]
+        plain = [keep.tile([P, S], F32, name=f"plain{t}") for t in range(PACK)]
+        for t in range(PACK):
+            nc.tensor.matmul_mx(
+                out=banks[t][:],
+                lhsT=w1d[:, 2 * P * t : 2 * P * (t + 1)].bitcast(FP4X4),
+                lhsT_scale=w1sd[:, P * t : P * (t + 1)],
+                rhs=qw[:].bitcast(FP8X4),
+                rhs_scale=qs[:],
+                start=True,
+                stop=True,
+            )
+            nc.scalar.activation(win[t][:, :S], banks[t][:], ACT.Copy, scale=neg_gain[:, t : t + 1])
+            nc.scalar.activation(plain[t][:], banks[t][:], ACT.Copy, scale=neg_gain[:, t : t + 1])
+
+        cas = dealt("casd", U8, gather("cas", U8, xs, l_ca, tag="w1w"))
+        cbs = dealt("cbsd", U8, gather("cbs", U8, xs, l_cb, tag="w1s"))
+        cbw = dealt("cbwd", U32, gather("cbw", U32, xw, l_cb, tag="w1s"))
+
+        den = keep.tile([P, PACK, S], F32)
+        num = keep.tile([P, PACK, S], F32)
+        rec = keep.tile([P, PACK, S], F32)
+        for t in range(PACK):
+            nc.vector.tensor_tensor(den[:, t, :], win[t][:].indirect(l_n2[:]), plain[t][:], ALU.subtract)
+        for t in range(PACK):
+            nc.vector.tensor_tensor(num[:, t, :], win[t][:].indirect(l_n1[:]), plain[t][:], ALU.subtract)
+        for t in range(PACK):
+            mag = ring.tile([P, S], F32, name="mag")
+            nc.scalar.activation(mag[:], den[:, t, :], ACT.Abs, scale=inv_gain[:, t : t + 1])
+            root = ring.tile([P, S], F32, name="root")
+            nc.scalar.activation(root[:], mag[:], ACT.Abs_reciprocal_sqrt, bias=half_c[:])
+            nc.scalar.activation(rec[:, t, :], root[:], ACT.Square)
+
+        zb = keep.tile([P, PACK * S], BF16, align_bytes=64, tag="zb")
+        nc.vector.tensor_tensor(woven(zb[:]), planes_walk(num[:]), planes_walk(rec[:]), ALU.mult)
+        zw = keep.tile([P, S], U32, align_bytes=64)
+        zs = keep.tile([P, S], U8, align_bytes=64)
+        nc.vector.quantize_mx(out=zw[:].bitcast(FP8X4), scales=zs[:], in_=zb[:])
+
+        caw = dealt("cawd", U32, gather("caw", U32, xw, l_ca, tag="zb"))
+
+        def score(bank, words, scales, t):
+            nc.tensor.matmul_mx(
+                out=bank[:],
+                lhsT=words[:, P * t : P * (t + 1)].bitcast(FP8X4),
+                lhsT_scale=scales[:, P * t : P * (t + 1)],
+                rhs=zw[:].bitcast(FP8X4),
+                rhs_scale=zs[:],
+                start=True,
+                stop=True,
+            )
+
+        prod = [keep.tile([P, S], F32, name=f"prod{t}") for t in range(PACK)]
+        for t in range(PACK):
+            bank = psum.tile([P, S], F32, name=f"b{t}", tag=f"b{t}")
+            score(bank, cbw, cbs, t)
+            th = keep.tile([P, S], F32, name=f"th{t}")
+            nc.scalar.activation(th[:], bank[:], ACT.Tanh, scale=0.0625)
+            nc.scalar.activation(win[t][:, :S], bank[:], ACT.Copy, scale=0.0625)
+            nc.vector.tensor_tensor(prod[t][:], win[t][:].indirect(l_n4[:]), th[:], ALU.mult)
+
+        awin = [keep.tile([P, S], F32, name=f"awin{t}") for t in range(PACK)]
+        for t in range(PACK):
+            bank = psum.tile([P, S], F32, name=f"a{t}", tag=f"ya{t}")
+            score(bank, caw, cas, t)
+            nc.scalar.activation(awin[t][:], bank[:], ACT.Copy, scale=0.0625)
+
+        out_rows = out_0.rearrange("(p t) j -> p t j", t=PACK)
+        out_words = out_1[0].rearrange("p n t -> p (n t)").bitcast(I32)
+        ow = keep.tile([P, S], U32, align_bytes=64)
+        osc = keep.tile([P, S], U8, align_bytes=64)
+        for h in range(2):
+            cols = slice(h * HALF, (h + 1) * HALF)
+            res = keep.tile([P, PACK, HALF], F32, name=f"res{h}")
+            for t in range(PACK):
+                nc.vector.tensor_tensor(
+                    res[:, t, :],
+                    awin[t][:].indirect(l_n3[:, h * HALF // 16 : (h + 1) * HALF // 16]),
+                    prod[t][:, cols],
+                    ALU.subtract,
+                )
+                if h == 1:
+                    nc.sync.dma_start(out=out_rows[:, t, cols], in_=res[:, t, :])
+            rb = keep.tile([P, PACK * HALF], BF16, name=f"rb{h}", align_bytes=64)
+            if h == 0:
+                nc.sync.dma_start(out=out_rows[:, :, cols], in_=res[:])
+                nc.scalar.copy(woven(rb[:]), planes_walk(res[:]))
+            else:
+                nc.vector.tensor_copy(woven(rb[:]), planes_walk(res[:]))
+            nc.vector.quantize_mx(out=ow[:, cols].bitcast(FP8X4), scales=osc[:, cols], in_=rb[:])
+            nc.sync.dma_start(out=out_words[:, cols], in_=ow[:, cols].bitcast(I32))
+        for q in range(QUADS):
+            queue = nc.scalar if q % 2 == 0 else nc.sync
+            queue.dma_start(
+                out=out_2[0, 4 * q : 4 * q + 4, :].bitcast(I32), in_=osc[32 * q : 32 * q + 4, :].bitcast(I32)
+            )

@@ -31,8 +31,8 @@ def load_scale_rows(queue, plane, rows):
 
 def deal(nc, dealt, plain):
     nc.vector.tensor_copy(
-        out=dealt.rearrange("p (t m) -> p t m", t=PACK),
-        in_=plain.rearrange("p (m t) -> p t m", t=PACK),
+        out=dealt.rearrange("p (t m) -> p m t", t=PACK),
+        in_=plain.rearrange("p (m t) -> p m t", t=PACK),
     )
 
 
@@ -62,19 +62,19 @@ def tile_picked_ccmpsoftbfrac_none_po_kernel(
         w1s = keep.tile([P, H], U8, align_bytes=64, tag="w1s")
         nc.vector.memset(xs[:].bitcast(I32), 0)
         nc.vector.memset(w1s[:].bitcast(I32), 0)
-        load_scale_rows(nc.scalar, xs, x_scales[0])
-        l_offs = list_tile("l_offs", offs)
         w1w = keep.tile([P, 2 * H], U8, align_bytes=64, tag="w1w")
         nc.sync.dma_start(out=w1w[:].bitcast(I32), in_=w1_words[0].bitcast(I32))
-        xw = keep.tile([P, T], U32, align_bytes=64)
-        nc.sync.dma_start(out=xw[:].bitcast(I32), in_=x_words[0].rearrange("p n t -> p (n t)").bitcast(I32))
-        l_ca = list_tile("l_ca", ca)
-        load_scale_rows(nc.scalar, w1s, w1_scales[0])
+        load_scale_rows(nc.sync, xs, x_scales[0])
+        l_offs = list_tile("l_offs", offs)
         gain = keep.tile([P, PACK], F32)
         nc.sync.dma_start(out=gain[:], in_=gs.rearrange("(p t) o -> p (t o)", t=PACK))
+        xw = keep.tile([P, T], U32, align_bytes=64)
+        nc.sync.dma_start(out=xw[:].bitcast(I32), in_=x_words[0].rearrange("p n t -> p (n t)").bitcast(I32))
+        load_scale_rows(nc.sync, w1s, w1_scales[0])
         l_cb = list_tile("l_cb", cb)
         l_n2 = list_tile("l_n2", n2)
         l_n1 = list_tile("l_n1", n1)
+        l_ca = list_tile("l_ca", ca)
         l_n4 = list_tile("l_n4", n4)
         l_n3 = list_tile("l_n3", n3)
 
@@ -89,21 +89,17 @@ def tile_picked_ccmpsoftbfrac_none_po_kernel(
             nc.vector.tensor_copy(out=g[:], in_=table[:].indirect(lst[:]))
             return g
 
+        def gather_dealt(name, table, lst, tag):
+            g = keep.tile([P, S], U32, name=name, align_bytes=64, tag=tag)
+            nc.vector.tensor_copy(out=g[:].rearrange("p (t m) -> p m t", t=PACK), in_=table[:].indirect(lst[:]))
+            return g
+
         def dealt(name, dtype, plain):
             d = keep.tile([P, S], dtype, name=name, align_bytes=64)
             deal(nc, d[:], plain[:])
             return d
 
-        qs = gather("qs", U8, xs, l_offs)
-        w1d = keep.tile([P, 2 * H], U8, align_bytes=64)
-        nc.vector.tensor_copy(
-            out=w1d[:].rearrange("p (t m b) -> p t m b", t=PACK, b=2),
-            in_=w1w[:].rearrange("p (m t b) -> p t m b", t=PACK, b=2),
-        )
-        w1sd = dealt("w1sd", U8, w1s)
-        qw = gather("qw", U32, xw, l_offs)
-
-        neg_gain = keep.tile([P, PACK], F32)
+        neg_gain = keep.tile([P, PACK], F32, tag="num", align_bytes=64)
         nc.vector.tensor_scalar(neg_gain[:], gain[:], -1.0, None, ALU.mult)
         abs_gain = keep.tile([P, PACK], F32)
         nc.vector.scalar_tensor_tensor(abs_gain[:], gain[:], TINY, neg_gain[:], ALU.max, ALU.max)
@@ -111,6 +107,15 @@ def tile_picked_ccmpsoftbfrac_none_po_kernel(
         nc.scalar.activation(root_gain[:], abs_gain[:], ACT.Abs_reciprocal_sqrt)
         inv_gain = keep.tile([P, PACK], F32)
         nc.scalar.activation(inv_gain[:], root_gain[:], ACT.Square)
+
+        qs = gather("qs", U8, xs, l_offs)
+        w1d = keep.tile([P, 2 * H], U8, align_bytes=64)
+        nc.vector.tensor_copy(
+            out=w1d[:].rearrange("p (t m b) -> p m t b", t=PACK, b=2),
+            in_=w1w[:].rearrange("p (m t b) -> p m t b", t=PACK, b=2),
+        )
+        w1sd = dealt("w1sd", U8, w1s)
+        qw = gather("qw", U32, xw, l_offs)
 
         banks = [psum.tile([P, S], F32, name=f"y{t}", tag=f"ya{t}") for t in range(PACK)]
         plain = [keep.tile([P, S], F32, name=f"plain{t}") for t in range(PACK)]
@@ -127,12 +132,11 @@ def tile_picked_ccmpsoftbfrac_none_po_kernel(
             nc.scalar.activation(win[t][:, :S], banks[t][:], ACT.Copy, scale=neg_gain[:, t : t + 1])
             nc.scalar.activation(plain[t][:], banks[t][:], ACT.Copy, scale=neg_gain[:, t : t + 1])
 
-        cas = dealt("casd", U8, gather("cas", U8, xs, l_ca, tag="w1w"))
         cbs = dealt("cbsd", U8, gather("cbs", U8, xs, l_cb, tag="w1s"))
-        cbw = dealt("cbwd", U32, gather("cbw", U32, xw, l_cb, tag="w1s"))
+        cbw = gather_dealt("cbw", xw, l_cb, "w1s")
 
         den = keep.tile([P, PACK, S], F32)
-        num = keep.tile([P, PACK, S], F32)
+        num = keep.tile([P, PACK, S], F32, tag="num", align_bytes=64)
         rec = keep.tile([P, PACK, S], F32)
         for t in range(PACK):
             nc.vector.tensor_tensor(den[:, t, :], win[t][:].indirect(l_n2[:]), plain[t][:], ALU.subtract)
@@ -151,7 +155,8 @@ def tile_picked_ccmpsoftbfrac_none_po_kernel(
         zs = keep.tile([P, S], U8, align_bytes=64)
         nc.vector.quantize_mx(out=zw[:].bitcast(FP8X4), scales=zs[:], in_=zb[:])
 
-        caw = dealt("cawd", U32, gather("caw", U32, xw, l_ca, tag="zb"))
+        caw = gather_dealt("caw", xw, l_ca, "zb")
+        cas = dealt("casd", U8, gather("cas", U8, xs, l_ca, tag="num"))
 
         def score(bank, words, scales, t):
             nc.tensor.matmul_mx(
@@ -164,7 +169,7 @@ def tile_picked_ccmpsoftbfrac_none_po_kernel(
                 stop=True,
             )
 
-        prod = [keep.tile([P, S], F32, name=f"prod{t}") for t in range(PACK)]
+        prod = [keep.tile([P, S], F32, name=f"prod{t}", align_bytes=64) for t in range(PACK)]
         for t in range(PACK):
             bank = psum.tile([P, S], F32, name=f"b{t}", tag=f"b{t}")
             score(bank, cbw, cbs, t)
@@ -181,27 +186,27 @@ def tile_picked_ccmpsoftbfrac_none_po_kernel(
 
         out_rows = out_0.rearrange("(p t) j -> p t j", t=PACK)
         out_words = out_1[0].rearrange("p n t -> p (n t)").bitcast(I32)
-        ow = keep.tile([P, S], U32, align_bytes=64)
         osc = keep.tile([P, S], U8, align_bytes=64)
-        for h in range(2):
-            cols = slice(h * HALF, (h + 1) * HALF)
-            res = keep.tile([P, PACK, HALF], F32, name=f"res{h}")
+        halves = [slice(h * HALF, (h + 1) * HALF) for h in range(2)]
+        res = [keep.tile([P, PACK, HALF], F32, name=f"res{h}") for h in range(2)]
+        rb = [keep.tile([P, PACK * HALF], BF16, name=f"rb{h}", align_bytes=64) for h in range(2)]
+        for h, cols in enumerate(halves):
             for t in range(PACK):
                 nc.vector.tensor_tensor(
-                    res[:, t, :],
+                    res[h][:, t, :],
                     awin[t][:].indirect(l_n3[:, h * HALF // 16 : (h + 1) * HALF // 16]),
                     prod[t][:, cols],
                     ALU.subtract,
                 )
                 if h == 1:
-                    nc.sync.dma_start(out=out_rows[:, t, cols], in_=res[:, t, :])
-            rb = keep.tile([P, PACK * HALF], BF16, name=f"rb{h}", align_bytes=64)
+                    nc.sync.dma_start(out=out_rows[:, t, cols], in_=res[h][:, t, :])
             if h == 0:
-                nc.sync.dma_start(out=out_rows[:, :, cols], in_=res[:])
-                nc.scalar.copy(woven(rb[:]), planes_walk(res[:]))
-            else:
-                nc.vector.tensor_copy(woven(rb[:]), planes_walk(res[:]))
-            nc.vector.quantize_mx(out=ow[:, cols].bitcast(FP8X4), scales=osc[:, cols], in_=rb[:])
+                nc.sync.dma_start(out=out_rows[:, :, cols], in_=res[h][:])
+                nc.scalar.copy(woven(rb[h][:]), planes_walk(res[h][:]))
+        ow = keep.tile([P, S], U32, align_bytes=64, tag=f"prod{PACK - 1}")
+        nc.vector.tensor_copy(woven(rb[1][:]), planes_walk(res[1][:]))
+        for h, cols in enumerate(halves):
+            nc.vector.quantize_mx(out=ow[:, cols].bitcast(FP8X4), scales=osc[:, cols], in_=rb[h][:])
             nc.sync.dma_start(out=out_words[:, cols], in_=ow[:, cols].bitcast(I32))
         for q in range(QUADS):
             queue = nc.scalar if q % 2 == 0 else nc.sync

@@ -20,6 +20,7 @@ P = 128
 PACK = 4
 QUADS = 4
 HALF = S // 2
+LAST = 128
 RUN = 4
 TINY = 1e-37
 
@@ -34,6 +35,14 @@ def deal(nc, dealt, plain):
         out=dealt.rearrange("p (t m) -> p m t", t=PACK),
         in_=plain.rearrange("p (m t) -> p m t", t=PACK),
     )
+
+
+def packed(cols):
+    return slice(PACK * cols.start, PACK * cols.stop)
+
+
+def entries(cols):
+    return slice(cols.start // 16, cols.stop // 16)
 
 
 def woven(ap):
@@ -66,15 +75,15 @@ def tile_picked_ccmpsoftbfrac_none_po_kernel(
         nc.sync.dma_start(out=w1w[:].bitcast(I32), in_=w1_words[0].bitcast(I32))
         load_scale_rows(nc.sync, xs, x_scales[0])
         l_offs = list_tile("l_offs", offs)
-        gain = keep.tile([P, PACK], F32)
-        nc.sync.dma_start(out=gain[:], in_=gs.rearrange("(p t) o -> p (t o)", t=PACK))
+        l_ca = list_tile("l_ca", ca)
         xw = keep.tile([P, T], U32, align_bytes=64)
         nc.sync.dma_start(out=xw[:].bitcast(I32), in_=x_words[0].rearrange("p n t -> p (n t)").bitcast(I32))
+        gain = keep.tile([P, PACK], F32)
+        nc.sync.dma_start(out=gain[:], in_=gs.rearrange("(p t) o -> p (t o)", t=PACK))
         load_scale_rows(nc.sync, w1s, w1_scales[0])
         l_cb = list_tile("l_cb", cb)
         l_n2 = list_tile("l_n2", n2)
         l_n1 = list_tile("l_n1", n1)
-        l_ca = list_tile("l_ca", ca)
         l_n4 = list_tile("l_n4", n4)
         l_n3 = list_tile("l_n3", n3)
 
@@ -94,8 +103,8 @@ def tile_picked_ccmpsoftbfrac_none_po_kernel(
             nc.vector.tensor_copy(out=g[:].rearrange("p (t m) -> p m t", t=PACK), in_=table[:].indirect(lst[:]))
             return g
 
-        def dealt(name, dtype, plain):
-            d = keep.tile([P, S], dtype, name=name, align_bytes=64)
+        def dealt(name, dtype, plain, tag=""):
+            d = keep.tile([P, S], dtype, name=name, align_bytes=64, tag=tag or name)
             deal(nc, d[:], plain[:])
             return d
 
@@ -118,7 +127,7 @@ def tile_picked_ccmpsoftbfrac_none_po_kernel(
         qw = gather("qw", U32, xw, l_offs)
 
         banks = [psum.tile([P, S], F32, name=f"y{t}", tag=f"ya{t}") for t in range(PACK)]
-        plain = [keep.tile([P, S], F32, name=f"plain{t}") for t in range(PACK)]
+        plain = [keep.tile([P, S], F32, name=f"plain{t}", align_bytes=64) for t in range(PACK)]
         for t in range(PACK):
             nc.tensor.matmul_mx(
                 out=banks[t][:],
@@ -132,8 +141,9 @@ def tile_picked_ccmpsoftbfrac_none_po_kernel(
             nc.scalar.activation(win[t][:, :S], banks[t][:], ACT.Copy, scale=neg_gain[:, t : t + 1])
             nc.scalar.activation(plain[t][:], banks[t][:], ACT.Copy, scale=neg_gain[:, t : t + 1])
 
-        cbs = dealt("cbsd", U8, gather("cbs", U8, xs, l_cb, tag="w1s"))
-        cbw = gather_dealt("cbw", xw, l_cb, "w1s")
+        cbs_plain = gather("cbs", U8, xs, l_cb, tag="w1s")
+        cbw = gather_dealt("cbw", xw, l_cb, "w1w")
+        cas_plain = gather("cas", U8, xs, l_ca)
 
         den = keep.tile([P, PACK, S], F32)
         num = keep.tile([P, PACK, S], F32, tag="num", align_bytes=64)
@@ -149,65 +159,82 @@ def tile_picked_ccmpsoftbfrac_none_po_kernel(
             nc.scalar.activation(root[:], mag[:], ACT.Abs_reciprocal_sqrt, bias=half_c[:])
             nc.scalar.activation(rec[:, t, :], root[:], ACT.Square)
 
+        cbs = dealt("cbsd", U8, cbs_plain, tag=f"plain{PACK - 2}")
+
         zb = keep.tile([P, PACK * S], BF16, align_bytes=64, tag="zb")
-        nc.vector.tensor_tensor(woven(zb[:]), planes_walk(num[:]), planes_walk(rec[:]), ALU.mult)
         zw = keep.tile([P, S], U32, align_bytes=64)
         zs = keep.tile([P, S], U8, align_bytes=64)
-        nc.vector.quantize_mx(out=zw[:].bitcast(FP8X4), scales=zs[:], in_=zb[:])
+        halves = [slice(h * HALF, (h + 1) * HALF) for h in range(2)]
+        for cols in halves:
+            nc.vector.tensor_tensor(
+                woven(zb[:, packed(cols)]), planes_walk(num[:, :, cols]), planes_walk(rec[:, :, cols]), ALU.mult
+            )
+        for cols in halves:
+            nc.vector.quantize_mx(out=zw[:, cols].bitcast(FP8X4), scales=zs[:, cols], in_=zb[:, packed(cols)])
 
         caw = gather_dealt("caw", xw, l_ca, "zb")
-        cas = dealt("casd", U8, gather("cas", U8, xs, l_ca, tag="num"))
+        cas = dealt("casd", U8, cas_plain, tag="num")
 
-        def score(bank, words, scales, t):
+        def score(bank, words, scales, t, cols):
             nc.tensor.matmul_mx(
-                out=bank[:],
+                out=bank,
                 lhsT=words[:, P * t : P * (t + 1)].bitcast(FP8X4),
                 lhsT_scale=scales[:, P * t : P * (t + 1)],
-                rhs=zw[:].bitcast(FP8X4),
-                rhs_scale=zs[:],
+                rhs=zw[:, cols].bitcast(FP8X4),
+                rhs_scale=zs[:, cols],
                 start=True,
                 stop=True,
             )
 
         prod = [keep.tile([P, S], F32, name=f"prod{t}", align_bytes=64) for t in range(PACK)]
         for t in range(PACK):
-            bank = psum.tile([P, S], F32, name=f"b{t}", tag=f"b{t}")
-            score(bank, cbw, cbs, t)
             th = keep.tile([P, S], F32, name=f"th{t}")
-            nc.scalar.activation(th[:], bank[:], ACT.Tanh, scale=0.0625)
-            nc.scalar.activation(win[t][:, :S], bank[:], ACT.Copy, scale=0.0625)
+            for n, cols in enumerate(halves if t == 0 else [slice(0, S)]):
+                bank = psum.tile([P, cols.stop - cols.start], F32, name=f"b{t}", tag=f"b{t}" if n == 0 else "ya3")
+                score(bank[:], cbw, cbs, t, cols)
+                nc.scalar.activation(th[:, cols], bank[:], ACT.Tanh, scale=0.0625)
+                nc.scalar.activation(win[t][:, cols], bank[:], ACT.Copy, scale=0.0625)
             nc.vector.tensor_tensor(prod[t][:], win[t][:].indirect(l_n4[:]), th[:], ALU.mult)
 
         awin = [keep.tile([P, S], F32, name=f"awin{t}") for t in range(PACK)]
         for t in range(PACK):
             bank = psum.tile([P, S], F32, name=f"a{t}", tag=f"ya{t}")
-            score(bank, caw, cas, t)
+            score(bank[:], caw, cas, t, slice(0, S))
+            nc.scalar.activation(win[t][:, :S], bank[:], ACT.Copy, scale=0.0625)
             nc.scalar.activation(awin[t][:], bank[:], ACT.Copy, scale=0.0625)
 
         out_rows = out_0.rearrange("(p t) j -> p t j", t=PACK)
         out_words = out_1[0].rearrange("p n t -> p (n t)").bitcast(I32)
         osc = keep.tile([P, S], U8, align_bytes=64)
-        halves = [slice(h * HALF, (h + 1) * HALF) for h in range(2)]
-        res = [keep.tile([P, PACK, HALF], F32, name=f"res{h}") for h in range(2)]
-        rb = [keep.tile([P, PACK * HALF], BF16, name=f"rb{h}", align_bytes=64) for h in range(2)]
-        for h, cols in enumerate(halves):
-            for t in range(PACK):
-                nc.vector.tensor_tensor(
-                    res[h][:, t, :],
-                    awin[t][:].indirect(l_n3[:, h * HALF // 16 : (h + 1) * HALF // 16]),
-                    prod[t][:, cols],
-                    ALU.subtract,
-                )
-                if h == 1:
-                    nc.sync.dma_start(out=out_rows[:, t, cols], in_=res[h][:, t, :])
-            if h == 0:
-                nc.sync.dma_start(out=out_rows[:, :, cols], in_=res[h][:])
-                nc.scalar.copy(woven(rb[h][:]), planes_walk(res[h][:]))
-        ow = keep.tile([P, S], U32, align_bytes=64, tag=f"prod{PACK - 1}")
-        nc.vector.tensor_copy(woven(rb[1][:]), planes_walk(res[1][:]))
-        for h, cols in enumerate(halves):
-            nc.vector.quantize_mx(out=ow[:, cols].bitcast(FP8X4), scales=osc[:, cols], in_=rb[h][:])
-            nc.sync.dma_start(out=out_words[:, cols], in_=ow[:, cols].bitcast(I32))
+        head, last = slice(0, S - LAST), slice(S - LAST, S)
+        res_head = keep.tile([P, PACK, S - LAST], F32)
+        res_last = keep.tile([P, PACK, LAST], F32)
+        pieces = [slice(0, HALF), slice(HALF, S - LAST), last]
+        rb = [keep.tile([P, PACK * (c.stop - c.start)], BF16, name=f"rb{n}", align_bytes=64) for n, c in enumerate(pieces)]
+        for t in range(PACK):
+            nc.vector.tensor_tensor(
+                res_head[:, t, :], win[t][:].indirect(l_n3[:, entries(head)]), prod[t][:, head], ALU.subtract
+            )
+            nc.sync.dma_start(out=out_rows[:, t, head], in_=res_head[:, t, :])
+        for n in range(2):
+            nc.scalar.copy(woven(rb[n][:]), planes_walk(res_head[:, :, pieces[n]]))
+        for t in range(PACK):
+            nc.vector.tensor_tensor(
+                res_last[:, t, :], awin[t][:].indirect(l_n3[:, entries(last)]), prod[t][:, last], ALU.subtract
+            )
+        nc.sync.dma_start(out=out_rows[:, :, last], in_=res_last[:])
+        ow = keep.tile([P, S], U32, align_bytes=64, tag=f"prod{PACK - 2}")
+
+        def hand_on(n):
+            cols = pieces[n]
+            nc.vector.quantize_mx(out=ow[:, cols].bitcast(FP8X4), scales=osc[:, cols], in_=rb[n][:])
+
+        hand_on(0)
+        nc.vector.tensor_copy(woven(rb[2][:]), planes_walk(res_last[:]))
+        hand_on(1)
+        hand_on(2)
+        nc.sync.dma_start(out=out_words[:, :HALF], in_=ow[:, :HALF].bitcast(I32))
+        nc.sync.dma_start(out=out_words[:, HALF:], in_=ow[:, HALF:].bitcast(I32))
         for q in range(QUADS):
             queue = nc.scalar if q % 2 == 0 else nc.sync
             queue.dma_start(

@@ -90,8 +90,7 @@ def tile_picked_ccmpsoftbfrac_none_po_kernel(
         half_c = keep.tile([P, 1], F32)
         nc.vector.memset(half_c[:], 0.5)
         win = [keep.tile([P, 2 * S], F32, name=f"win{t}") for t in range(PACK)]
-        for t in range(PACK):
-            nc.vector.memset(win[t][:, S:], 0.0)
+        nc.vector.memset(win[0][:, S:], 0.0)
 
         def gather(name, dtype, table, lst, tag=""):
             g = keep.tile([P, S], dtype, name=name, align_bytes=64, tag=tag or name)
@@ -119,15 +118,19 @@ def tile_picked_ccmpsoftbfrac_none_po_kernel(
 
         qs = gather("qs", U8, xs, l_offs)
         w1d = keep.tile([P, 2 * H], U8, align_bytes=64)
-        nc.vector.tensor_copy(
-            out=w1d[:].rearrange("p (t m b) -> p m t b", t=PACK, b=2),
-            in_=w1w[:].rearrange("p (m t b) -> p m t b", t=PACK, b=2),
+        nc.gpsimd.tensor_copy(
+            out=w1d[:].rearrange("p (t m b) -> p t m b", t=PACK, b=2),
+            in_=w1w[:].rearrange("p (m t b) -> p t m b", t=PACK, b=2),
         )
-        w1sd = dealt("w1sd", U8, w1s)
+        w1sd = keep.tile([P, H], U8, align_bytes=64)
+        nc.gpsimd.tensor_copy(
+            out=w1sd[:].rearrange("p (t m) -> p t m", t=PACK), in_=w1s[:].rearrange("p (m t) -> p t m", t=PACK)
+        )
         qw = gather("qw", U32, xw, l_offs)
 
         banks = [psum.tile([P, S], F32, name=f"y{t}", tag=f"ya{t}") for t in range(PACK)]
-        plain = [keep.tile([P, S], F32, name=f"plain{t}", align_bytes=64) for t in range(PACK)]
+        plain_last = keep.tile([P, S], F32, align_bytes=64, tag="plain_last")
+        plain = [win[t + 1][:, S:] for t in range(PACK - 1)] + [plain_last[:]]
         for t in range(PACK):
             nc.tensor.matmul_mx(
                 out=banks[t][:],
@@ -139,19 +142,19 @@ def tile_picked_ccmpsoftbfrac_none_po_kernel(
                 stop=True,
             )
             nc.scalar.activation(win[t][:, :S], banks[t][:], ACT.Copy, scale=neg_gain[:, t : t + 1])
-            nc.scalar.activation(plain[t][:], banks[t][:], ACT.Copy, scale=neg_gain[:, t : t + 1])
+            nc.scalar.activation(plain[t], banks[t][:], ACT.Copy, scale=neg_gain[:, t : t + 1])
 
-        cbs_plain = gather("cbs", U8, xs, l_cb, tag="w1s")
-        cbw = gather_dealt("cbw", xw, l_cb, "w1w")
+        cbs_plain = gather("cbs", U8, xs, l_cb)
+        cbw = gather_dealt("cbw", xw, l_cb, "cbw")
         cas_plain = gather("cas", U8, xs, l_ca)
 
         den = keep.tile([P, PACK, S], F32)
         num = keep.tile([P, PACK, S], F32, tag="num", align_bytes=64)
         rec = keep.tile([P, PACK, S], F32)
         for t in range(PACK):
-            nc.vector.tensor_tensor(den[:, t, :], win[t][:].indirect(l_n2[:]), plain[t][:], ALU.subtract)
-        for t in range(PACK):
-            nc.vector.tensor_tensor(num[:, t, :], win[t][:].indirect(l_n1[:]), plain[t][:], ALU.subtract)
+            nc.vector.tensor_tensor(den[:, t, :], win[t][:].indirect(l_n2[:]), plain[t], ALU.subtract)
+        for t in reversed(range(PACK)):
+            nc.vector.tensor_tensor(num[:, t, :], win[t][:].indirect(l_n1[:]), plain[t], ALU.subtract)
         for t in range(PACK):
             mag = ring.tile([P, S], F32, name="mag")
             nc.scalar.activation(mag[:], den[:, t, :], ACT.Abs, scale=inv_gain[:, t : t + 1])
@@ -159,7 +162,7 @@ def tile_picked_ccmpsoftbfrac_none_po_kernel(
             nc.scalar.activation(root[:], mag[:], ACT.Abs_reciprocal_sqrt, bias=half_c[:])
             nc.scalar.activation(rec[:, t, :], root[:], ACT.Square)
 
-        cbs = dealt("cbsd", U8, cbs_plain, tag=f"plain{PACK - 2}")
+        cbs = dealt("cbsd", U8, cbs_plain, tag="plain_last")
 
         zb = keep.tile([P, PACK * S], BF16, align_bytes=64, tag="zb")
         zw = keep.tile([P, S], U32, align_bytes=64)

from contextlib import ExitStack

import concourse.mybir as mybir

K, T, S, H, C = 512, 2048, 512, 512, 512
FLOPS = 2 * K * H * S + 2 * 2 * K * C * S

F32 = mybir.dt.float32
BF16 = mybir.dt.bfloat16
I32 = mybir.dt.int32
U32 = mybir.dt.uint32
U16 = mybir.dt.uint16
U8 = mybir.dt.uint8
FP8X4 = mybir.dt.float8_e4m3fn_x4
FP4X4 = mybir.dt.float4_e2m1fn_x4
ALU = mybir.AluOpType
ACT = mybir.ActivationFunctionType

P = 128
PACK = 4
QUADS = 4
HALF = S // 2
LAST = 128
RUN = 4
TINY = 1e-37


def load_scale_rows(queue, plane, rows):
    for q in range(QUADS):
        queue.dma_start(out=plane[32 * q : 32 * q + 4, :].bitcast(I32), in_=rows[4 * q : 4 * q + 4, :].bitcast(I32))


def deal(nc, dealt, plain):
    nc.vector.tensor_copy(
        out=dealt.rearrange("p (t m) -> p m t", t=PACK),
        in_=plain.rearrange("p (m t) -> p m t", t=PACK),
    )


def packed(cols):
    return slice(PACK * cols.start, PACK * cols.stop)


def entries(cols):
    return slice(cols.start // 16, cols.stop // 16)


def woven(ap):
    return ap.rearrange("p (c i t) -> p c t i", i=RUN, t=PACK)


def planes_walk(ap):
    return ap.rearrange("p t (c i) -> p c t i", i=RUN)


def tile_picked_ccmpsoftbfrac_none_po_kernel(
    tc, x_words, x_scales, w1_words, w1_scales, gs, offs, n1, n2, ca, cb, n3, n4, out_0, out_1, out_2
):
    nc = tc.nc
    with ExitStack() as ctx:
        keep = ctx.enter_context(tc.tile_pool(name="keep", bufs=1))
        ring = ctx.enter_context(tc.tile_pool(name="ring", bufs=2))
        psum = ctx.enter_context(tc.psum_pool(name="psum", bufs=1))

        def list_tile(name, src):
            t = keep.tile([P, S // 16], U16, name=name)
            nc.sync.dma_start(t[:], src)
            return t

        xs = keep.tile([P, T], U8, align_bytes=64)
        w1s = keep.tile([P, H], U8, align_bytes=64, tag="w1s")
        nc.vector.memset(xs[:].bitcast(I32), 0)
        nc.vector.memset(w1s[:].bitcast(I32), 0)
        w1w = keep.tile([P, 2 * H], U8, align_bytes=64, tag="w1w")
        nc.sync.dma_start(out=w1w[:].bitcast(I32), in_=w1_words[0].bitcast(I32))
        load_scale_rows(nc.sync, xs, x_scales[0])
        l_offs = list_tile("l_offs", offs)
        l_ca = list_tile("l_ca", ca)
        xw = keep.tile([P, T], U32, align_bytes=64)
        nc.sync.dma_start(out=xw[:].bitcast(I32), in_=x_words[0].rearrange("p n t -> p (n t)").bitcast(I32))
        gain = keep.tile([P, PACK], F32)
        nc.sync.dma_start(out=gain[:], in_=gs.rearrange("(p t) o -> p (t o)", t=PACK))
        load_scale_rows(nc.sync, w1s, w1_scales[0])
        l_cb = list_tile("l_cb", cb)
        l_n2 = list_tile("l_n2", n2)
        l_n1 = list_tile("l_n1", n1)
        l_n4 = list_tile("l_n4", n4)
        l_n3 = list_tile("l_n3", n3)

        half_c = keep.tile([P, 1], F32)
        nc.vector.memset(half_c[:], 0.5)
        win = [keep.tile([P, 2 * S], F32, name=f"win{t}") for t in range(PACK)]
        nc.vector.memset(win[0][:, S:], 0.0)

        def gather(name, dtype, table, lst, tag=""):
            g = keep.tile([P, S], dtype, name=name, align_bytes=64, tag=tag or name)
            nc.vector.tensor_copy(out=g[:], in_=table[:].indirect(lst[:]))
            return g

        def gather_dealt(name, table, lst, tag):
            g = keep.tile([P, S], U32, name=name, align_bytes=64, tag=tag)
            nc.vector.tensor_copy(out=g[:].rearrange("p (t m) -> p m t", t=PACK), in_=table[:].indirect(lst[:]))
            return g

        def dealt(name, dtype, plain, tag=""):
            d = keep.tile([P, S], dtype, name=name, align_bytes=64, tag=tag or name)
            deal(nc, d[:], plain[:])
            return d

        neg_gain = keep.tile([P, PACK], F32, tag="num", align_bytes=64)
        nc.vector.tensor_scalar(neg_gain[:], gain[:], -1.0, None, ALU.mult)
        abs_gain = keep.tile([P, PACK], F32)
        nc.vector.scalar_tensor_tensor(abs_gain[:], gain[:], TINY, neg_gain[:], ALU.max, ALU.max)
        root_gain = keep.tile([P, PACK], F32)
        nc.scalar.activation(root_gain[:], abs_gain[:], ACT.Abs_reciprocal_sqrt)
        inv_gain = keep.tile([P, PACK], F32)
        nc.scalar.activation(inv_gain[:], root_gain[:], ACT.Square)

        qs = gather("qs", U8, xs, l_offs)
        w1d = keep.tile([P, 2 * H], U8, align_bytes=64)
        nc.gpsimd.tensor_copy(
            out=w1d[:].rearrange("p (t m b) -> p t m b", t=PACK, b=2),
            in_=w1w[:].rearrange("p (m t b) -> p t m b", t=PACK, b=2),
        )
        w1sd = keep.tile([P, H], U8, align_bytes=64)
        nc.gpsimd.tensor_copy(
            out=w1sd[:].rearrange("p (t m) -> p t m", t=PACK), in_=w1s[:].rearrange("p (m t) -> p t m", t=PACK)
        )
        qw = gather("qw", U32, xw, l_offs)

        banks = [psum.tile([P, S], F32, name=f"y{t}", tag=f"ya{t}") for t in range(PACK)]
        plain_last = keep.tile([P, S], F32, align_bytes=64, tag="plain_last")
        plain = [win[t + 1][:, S:] for t in range(PACK - 1)] + [plain_last[:]]
        for t in range(PACK):
            nc.tensor.matmul_mx(
                out=banks[t][:],
                lhsT=w1d[:, 2 * P * t : 2 * P * (t + 1)].bitcast(FP4X4),
                lhsT_scale=w1sd[:, P * t : P * (t + 1)],
                rhs=qw[:].bitcast(FP8X4),
                rhs_scale=qs[:],
                start=True,
                stop=True,
            )
            nc.scalar.activation(win[t][:, :S], banks[t][:], ACT.Copy, scale=neg_gain[:, t : t + 1])
            nc.scalar.activation(plain[t], banks[t][:], ACT.Copy, scale=neg_gain[:, t : t + 1])

        cbs_plain = gather("cbs", U8, xs, l_cb)
        cbw = gather_dealt("cbw", xw, l_cb, "cbw")
        cas_plain = gather("cas", U8, xs, l_ca)

        den = keep.tile([P, PACK, S], F32)
        num = keep.tile([P, PACK, S], F32, tag="num", align_bytes=64)
        rec = keep.tile([P, PACK, S], F32)
        for t in range(PACK):
            nc.vector.tensor_tensor(den[:, t, :], win[t][:].indirect(l_n2[:]), plain[t], ALU.subtract)
        for t in reversed(range(PACK)):
            nc.vector.tensor_tensor(num[:, t, :], win[t][:].indirect(l_n1[:]), plain[t], ALU.subtract)
        for t in range(PACK):
            mag = ring.tile([P, S], F32, name="mag")
            nc.scalar.activation(mag[:], den[:, t, :], ACT.Abs, scale=inv_gain[:, t : t + 1])
            root = ring.tile([P, S], F32, name="root")
            nc.scalar.activation(root[:], mag[:], ACT.Abs_reciprocal_sqrt, bias=half_c[:])
            nc.scalar.activation(rec[:, t, :], root[:], ACT.Square)

        cbs = dealt("cbsd", U8, cbs_plain, tag="plain_last")

        zb = keep.tile([P, PACK * S], BF16, align_bytes=64, tag="zb")
        zw = keep.tile([P, S], U32, align_bytes=64)
        zs = keep.tile([P, S], U8, align_bytes=64)
        halves = [slice(h * HALF, (h + 1) * HALF) for h in range(2)]
        for cols in halves:
            nc.vector.tensor_tensor(
                woven(zb[:, packed(cols)]), planes_walk(num[:, :, cols]), planes_walk(rec[:, :, cols]), ALU.mult
            )
        for cols in halves:
            nc.vector.quantize_mx(out=zw[:, cols].bitcast(FP8X4), scales=zs[:, cols], in_=zb[:, packed(cols)])

        caw = gather_dealt("caw", xw, l_ca, "zb")
        cas = dealt("casd", U8, cas_plain, tag="num")

        def score(bank, words, scales, t, cols):
            nc.tensor.matmul_mx(
                out=bank,
                lhsT=words[:, P * t : P * (t + 1)].bitcast(FP8X4),
                lhsT_scale=scales[:, P * t : P * (t + 1)],
                rhs=zw[:, cols].bitcast(FP8X4),
                rhs_scale=zs[:, cols],
                start=True,
                stop=True,
            )

        prod = [keep.tile([P, S], F32, name=f"prod{t}", align_bytes=64) for t in range(PACK)]
        for t in range(PACK):
            th = keep.tile([P, S], F32, name=f"th{t}")
            for n, cols in enumerate(halves if t == 0 else [slice(0, S)]):
                bank = psum.tile([P, cols.stop - cols.start], F32, name=f"b{t}", tag=f"b{t}" if n == 0 else "ya3")
                score(bank[:], cbw, cbs, t, cols)
                nc.scalar.activation(th[:, cols], bank[:], ACT.Tanh, scale=0.0625)
                nc.scalar.activation(win[t][:, cols], bank[:], ACT.Copy, scale=0.0625)
            nc.vector.tensor_tensor(prod[t][:], win[t][:].indirect(l_n4[:]), th[:], ALU.mult)

        awin = [keep.tile([P, S], F32, name=f"awin{t}") for t in range(PACK)]
        for t in range(PACK):
            bank = psum.tile([P, S], F32, name=f"a{t}", tag=f"ya{t}")
            score(bank[:], caw, cas, t, slice(0, S))
            nc.scalar.activation(win[t][:, :S], bank[:], ACT.Copy, scale=0.0625)
            nc.scalar.activation(awin[t][:], bank[:], ACT.Copy, scale=0.0625)

        out_rows = out_0.rearrange("(p t) j -> p t j", t=PACK)
        out_words = out_1[0].rearrange("p n t -> p (n t)").bitcast(I32)
        osc = keep.tile([P, S], U8, align_bytes=64)
        head, last = slice(0, S - LAST), slice(S - LAST, S)
        res_head = keep.tile([P, PACK, S - LAST], F32)
        res_last = keep.tile([P, PACK, LAST], F32)
        pieces = [slice(0, HALF), slice(HALF, S - LAST), last]
        rb = [keep.tile([P, PACK * (c.stop - c.start)], BF16, name=f"rb{n}", align_bytes=64) for n, c in enumerate(pieces)]
        for t in range(PACK):
            nc.vector.tensor_tensor(
                res_head[:, t, :], win[t][:].indirect(l_n3[:, entries(head)]), prod[t][:, head], ALU.subtract
            )
            nc.sync.dma_start(out=out_rows[:, t, head], in_=res_head[:, t, :])
        for n in range(2):
            nc.scalar.copy(woven(rb[n][:]), planes_walk(res_head[:, :, pieces[n]]))
        for t in range(PACK):
            nc.vector.tensor_tensor(
                res_last[:, t, :], awin[t][:].indirect(l_n3[:, entries(last)]), prod[t][:, last], ALU.subtract
            )
        nc.sync.dma_start(out=out_rows[:, :, last], in_=res_last[:])
        ow = keep.tile([P, S], U32, align_bytes=64, tag=f"prod{PACK - 2}")

        def hand_on(n):
            cols = pieces[n]
            nc.vector.quantize_mx(out=ow[:, cols].bitcast(FP8X4), scales=osc[:, cols], in_=rb[n][:])

        hand_on(0)
        nc.vector.tensor_copy(woven(rb[2][:]), planes_walk(res_last[:]))
        hand_on(1)
        hand_on(2)
        nc.sync.dma_start(out=out_words[:, :HALF], in_=ow[:, :HALF].bitcast(I32))
        nc.sync.dma_start(out=out_words[:, HALF:], in_=ow[:, HALF:].bitcast(I32))
        for q in range(QUADS):
            queue = nc.scalar if q % 2 == 0 else nc.sync
            queue.dma_start(
                out=out_2[0, 4 * q : 4 * q + 4, :].bitcast(I32), in_=osc[32 * q : 32 * q + 4, :].bitcast(I32)
            )
